import numpy as np
import ml_dtypes


def mxq(x, axis, fmt="e4m3"):
    dtype, down = {"e4m3": (ml_dtypes.float8_e4m3fn, 7), "e5m2": (ml_dtypes.float8_e5m2, 14)}[fmt]
    v = np.moveaxis(np.asarray(x, np.float32).astype(ml_dtypes.bfloat16).astype(np.float64), axis, -1)
    blocks = v.reshape(v.shape[:-1] + (-1, 32))
    amax = np.abs(blocks).max(-1, keepdims=True)
    byte = np.maximum(np.where(amax > 0, np.frexp(amax)[1] - 1 + 127, 0) - down, 1)
    scale = np.exp2(byte - 127.0)
    codes = (blocks / scale).astype(np.float32).astype(dtype).astype(np.float64)
    return np.moveaxis((codes * scale).reshape(v.shape), -1, axis)


WIDE = False


def mx_kscale(k):
    if not WIDE:
        return np.ones(k)
    levels = np.array([10, -10, 5, -5, 0])
    if k % 512:
        return np.exp2(np.random.permutation(np.resize(levels, k // 32))).repeat(32)
    a = np.empty((k // 512, 16))
    for p in range(k // 512):
        a[p, :8] = np.random.permutation(np.resize(levels, 8))
        for g in range(8):
            far = levels[np.abs(levels - a[p, g]) >= 10]
            a[p, g + 8] = far[np.random.randint(len(far))]
    return np.exp2(a.ravel()).repeat(32)


def f64(x):
    return np.asarray(x).astype(np.float64)


def striped(idx):
    return np.tile(np.asarray(idx).reshape(-1, 16).T, (8, 1)).astype(np.uint16)


def unstriped(offs):
    return offs[:16].T.reshape(-1).astype(np.int64)


E2M1 = np.array([0.0, 0.5, 1.0, 1.5, 2.0, 3.0, 4.0, 6.0, -0.0, -0.5, -1.0, -1.5, -2.0, -3.0, -4.0, -6.0])


def pack_weight(w, fmt):
    k, n = w.shape
    w = f64(np.asarray(w, np.float32).astype(ml_dtypes.bfloat16)).reshape(k // 32, 32, n)
    amax = np.abs(w).max(1)
    if fmt == "e4m3":
        byte = np.frexp(amax)[1] - 1 + 127 - 7
    else:
        mant, ex = np.frexp(amax / 6.0)
        byte = np.where(mant > 0.5, ex, ex - 1) + 127
    byte = np.clip(np.where(amax > 0, byte, 1), 1, 254)
    scaled = (w * np.exp2(127.0 - byte)[:, None, :]).reshape(k, n).astype(np.float32)
    by_word = np.ascontiguousarray(scaled.reshape(k // 512, 128, 4, n).transpose(0, 1, 3, 2))
    if fmt == "e4m3":
        words = by_word.astype(ml_dtypes.float8_e4m3fn).view(np.uint8)
    else:
        c = by_word.astype(ml_dtypes.float4_e2m1fn).view(np.uint8) & 0xF
        words = (c[..., 0::2] | (c[..., 1::2] << 4)).reshape(k // 512, 128, 2 * n)
    return np.ascontiguousarray(words), np.ascontiguousarray(byte.astype(np.uint8).reshape(k // 512, 16, n))


def unpack_weight(words, scales, fmt):
    g, _, n = scales.shape
    words = np.ascontiguousarray(words).reshape(g, 128, n, -1)
    if fmt == "e4m3":
        vals = words.view(ml_dtypes.float8_e4m3fn).astype(np.float64)
    else:
        nib = np.empty((g, 128, n, 4), np.uint8)
        nib[..., 0::2] = words & 0xF
        nib[..., 1::2] = words >> 4
        vals = E2M1[nib]
    vals = vals * np.repeat(np.exp2(scales.astype(np.float64) - 127.0), 8, axis=1)[..., None]
    return vals.transpose(0, 1, 3, 2).reshape(g * 512, n)


def sigmoid(v):
    return 1.0 / (1.0 + np.exp(-v))


def bf(x):
    return np.asarray(x, np.float32).astype(ml_dtypes.bfloat16)


def planes(Y):
    r, m = Y.shape
    b = f64(bf(Y)).reshape(r // 32, 32, m)
    amax = np.abs(b).max(1)
    byte = np.clip(np.where(amax > 0, np.frexp(amax)[1] - 1 + 127 - 7, 1), 1, 254)
    codes = (b * np.exp2(127.0 - byte)[:, None, :]).reshape(r, m).astype(np.float32).astype(ml_dtypes.float8_e4m3fn).view(np.uint8)
    words = codes.reshape(r // 512, 128, 4, m).transpose(0, 1, 3, 2)
    return np.ascontiguousarray(words), np.ascontiguousarray(byte.astype(np.uint8).reshape(r // 512, 16, m))


D, E, T, I, Q = 512, 512, 2048, 512, 256


def setup_inputs():
    n = np.random.standard_normal
    idx = np.random.permutation(T)[:I]
    fd = mx_kscale(D)
    fi = mx_kscale(I)
    ti = np.ones(T)
    ti[idx] = fi
    keysp = pack_weight(n((D, T)) / fd[:, None], "e4m3")
    return {
        "query": (n((D, Q)) * 0.8 / np.sqrt(D) * fd[:, None]).astype(np.float32),
        "keys_words": keysp[0],
        "keys_scales": keysp[1],
        "th": (np.random.uniform(0.4, 1.0, (Q, 1))).astype(np.float32),
        "os": (np.random.uniform(4.0, 16.0, (1, I)) * fi).astype(np.float32),
        "vals": (n((E, T)) / ti).astype(np.float32),
        "offs": striped(idx),
    }


def reference(query, keys_words, keys_scales, th, os, vals, offs):
    idx = unstriped(offs)
    keysu = unpack_weight(keys_words, keys_scales, "e4m3")
    queryq = mxq(f64(query), 0, "e4m3")
    keysidxg = keysu[:, idx]
    a = queryq.T @ keysidxg
    e1s = sigmoid((f64(th) - np.mean(np.square(a), axis=1, keepdims=True)) * 4.0)
    p = np.exp(a - np.max(a, axis=1, keepdims=True))
    z = np.sum(p, axis=1, keepdims=True)
    w = p / z * (1.0 - e1s) + e1s / 512.0
    wo1 = w * f64(os)
    wt1 = wo1.T
    vt1 = f64(vals)[:, idx].T
    vt1q = mxq(vt1, 0, "e4m3")
    wt1q = mxq(wt1, 0, "e4m3")
    o = vt1q.T @ wt1q
    words, scales = planes(o)
    return o, words, scales

@@ -1,0 +1,242 @@
+from contextlib import ExitStack
+
+import concourse.mybir as mybir
+from concourse.masks import make_identity
+
+D, E, T, SLOTS, Q = 512, 512, 2048, 512, 256
+FLOPS = 2 * D * Q * SLOTS + 2 * SLOTS * E * Q
+
+F32 = mybir.dt.float32
+BF16 = mybir.dt.bfloat16
+I32 = mybir.dt.int32
+U32 = mybir.dt.uint32
+U16 = mybir.dt.uint16
+U8 = mybir.dt.uint8
+FP8X4 = mybir.dt.float8_e4m3fn_x4
+ACT = mybir.ActivationFunctionType
+ALU = mybir.AluOpType
+AX = mybir.AxisListType
+
+P = 128
+PACK = 4
+HALVES = Q // P
+EARLY = 2
+
+
+def tile_attend_evenbyspread_pl_kernel(tc, query, keys_words, keys_scales, th, slot_factor, vals, offs, out_0, out_1, out_2):
+    nc = tc.nc
+    with ExitStack() as ctx:
+        sb = ctx.enter_context(tc.tile_pool(name="sb", bufs=1))
+        ps = ctx.enter_context(tc.psum_pool(name="ps", bufs=1))
+        ring = ctx.enter_context(tc.psum_pool(name="ring", bufs=2))
+
+        offsets = sb.tile([P, SLOTS // 16], U16, name="offsets")
+        key_scale_pool = sb.tile([P, T], U8, name="key_scale_pool", align_bytes=64)
+        key_word_pool = sb.tile([P, T], I32, name="key_word_pool", align_bytes=64)
+        query_raw = sb.tile([P, PACK, Q], F32, name="query_raw", align_bytes=64)
+        value_pools = [sb.tile([P, T], F32, name=f"value_pool{t}", tag=f"slot_v{t}", align_bytes=64) for t in range(PACK)]
+        th_cols = sb.tile([P, HALVES], F32, name="th_cols")
+        os_cols = sb.tile([P, PACK], F32, name="os_cols")
+        identity = sb.tile([P, P], F32, name="identity")
+        warm = sb.tile([P, 1], F32, name="warm")
+
+        vals_dealt = vals.rearrange("(p t) c -> p t c", t=PACK)
+        nc.vector.memset(key_scale_pool[:].bitcast(I32), 0)
+        make_identity(nc, identity[:])
+        nc.sync.dma_start(out=query_raw[:], in_=query.rearrange("(p j) q -> p j q", j=PACK))
+        nc.sync.dma_start(offsets[:], offs)
+        for quad in range(4):
+            nc.sync.dma_start(
+                out=key_scale_pool[32 * quad : 32 * quad + 4, :].bitcast(I32),
+                in_=keys_scales[0, 4 * quad : 4 * quad + 4, :].bitcast(I32),
+            )
+        nc.sync.dma_start(out=key_word_pool[:], in_=keys_words[0].rearrange("p t r -> p (t r)").bitcast(I32))
+        nc.sync.dma_start(out=value_pools[0][:], in_=vals_dealt[:, 0, :])
+        with nc.allow_non_contiguous_dma(reason="one threshold a partition"):
+            nc.sync.dma_start(out=th_cols[:], in_=th.rearrange("(b p) o -> p (b o)", p=P))
+        nc.sync.dma_start(out=value_pools[1][:], in_=vals_dealt[:, 1, :])
+        nc.sync.dma_start(out=os_cols[:], in_=slot_factor.rearrange("o (s r) -> s (o r)", r=PACK))
+        for t in range(2, PACK):
+            nc.sync.dma_start(out=value_pools[t][:], in_=vals_dealt[:, t, :])
+        nc.scalar.activation(warm[:], identity[:, 0:1], ACT.Exp)
+
+        key_scales = sb.tile([P, SLOTS], U8, name="key_scales", align_bytes=64)
+        key_words = sb.tile([P, SLOTS], U32, name="key_words", tag="slot_k", align_bytes=64)
+        nc.vector.tensor_copy(key_scales[:], key_scale_pool[:].indirect(offsets[:]))
+
+        query_grouped = sb.tile([P, Q, PACK], BF16, name="query_grouped", align_bytes=64)
+        query_codes = sb.tile([P, Q], U32, name="query_codes", align_bytes=64)
+        query_scales = sb.tile([P, Q], U8, name="query_scales", align_bytes=64)
+        nc.scalar.copy(query_grouped[:], query_raw[:].rearrange("p j q -> p q j"))
+        nc.vector.quantize_mx(
+            out=query_codes[:].bitcast(FP8X4), scales=query_scales[:], in_=query_grouped[:].rearrange("p q j -> p (q j)")
+        )
+        scores = [ps.tile([P, SLOTS], F32, name=f"scores{b}") for b in range(HALVES)]
+        run = SLOTS // 2
+        for h in range(2):
+            slots = slice(h * run, (h + 1) * run)
+            nc.vector.tensor_copy(
+                key_words[:, slots], key_word_pool[:].bitcast(U32).indirect(offsets[:, h * run // 16 : (h + 1) * run // 16])
+            )
+            for b in range(HALVES):
+                cols = slice(b * P, (b + 1) * P)
+                nc.tensor.matmul_mx(
+                    out=scores[b][:, slots],
+                    lhsT=query_codes[:, cols].bitcast(FP8X4),
+                    lhsT_scale=query_scales[:, cols],
+                    rhs=key_words[:, slots].bitcast(FP8X4),
+                    rhs_scale=key_scales[:, slots],
+                    start=True,
+                    stop=True,
+                )
+
+        results = [ps.tile([P, PACK, P], F32, name=f"results{b}") for b in range(HALVES)]
+        value_grouped = {j: sb.tile([P, 1, P, 2], F32, name=f"value_grouped{j}", align_bytes=64) for j in (1, 2)}
+        place = [(0, 0), (0, 1), (1, 0), (2, 0)]
+
+        def pick_and_turn(t, tag):
+            picked = sb.tile([P, SLOTS], BF16, name=f"picked{t}", tag=tag, align_bytes=64)
+            nc.vector.tensor_copy(picked[:], value_pools[t][:].indirect(offsets[:]))
+            pairs = picked[:].bitcast(F32)
+            turned_values = ring.tile([P, 2, P], F32, name="turned_values")
+            for u in range(2):
+                nc.tensor.transpose(turned_values[:, u, :], pairs[:, u : SLOTS // 2 : 2], identity[:])
+            j, n = place[t]
+            nc.scalar.copy(value_grouped[j][:, n, :, :], turned_values[:].rearrange("s u m -> s m u"))
+
+        neg_max = [sb.tile([P, 1], F32, name=f"neg_max{b}", tag=f"slot_m{b}", align_bytes=64) for b in range(HALVES)]
+        square_sum = sb.tile([P, HALVES], F32, name="square_sum")
+        exp_sum = sb.tile([P, HALVES], F32, name="exp_sum")
+        tilt = sb.tile([P, HALVES], F32, name="tilt")
+        softmax_share = sb.tile([P, HALVES], F32, name="softmax_share")
+        even_share = sb.tile([P, HALVES], F32, name="even_share")
+        gain = sb.tile([P, HALVES], F32, name="gain")
+        exps = [sb.tile([P, PACK, P], F32, name=f"exps{b}", tag=f"slot_e{b}", align_bytes=64) for b in range(HALVES)]
+        weights = [sb.tile([P, PACK, P], F32, name=f"weights{b}", tag=f"slot_w{b}", align_bytes=64) for b in range(HALVES)]
+
+        def square(b):
+            nc.scalar.activation(
+                weights[b][:].rearrange("p r s -> p (r s)"),
+                scores[b][:],
+                ACT.Square,
+                scale=1.0 / 16.0,
+                accum_out=square_sum[:, b : b + 1],
+            )
+            nc.scalar.activation(
+                tilt[:, b : b + 1], th_cols[:, b : b + 1], ACT.Tanh, scale=-2.0, bias=square_sum[:, b : b + 1]
+            )
+
+        def exponent(b):
+            nc.scalar.activation(
+                exps[b][:],
+                scores[b][:].rearrange("p (s r) -> p r s", r=PACK),
+                ACT.Exp,
+                bias=neg_max[b][:],
+                accum_out=exp_sum[:, b : b + 1],
+            )
+
+        inv_sum = sb.tile([P, HALVES], F32, name="inv_sum", tag="slot_r", align_bytes=64)
+        nc.vector.tensor_reduce(neg_max[0][:], scores[0][:], AX.X, ALU.max, negate=True)
+        square(1)
+        nc.vector.tensor_reduce(neg_max[1][:], scores[1][:], AX.X, ALU.max, negate=True)
+        exponent(0)
+        nc.vector.reciprocal(inv_sum[:, 0:1], exp_sum[:, 0:1])
+        square(0)
+        exponent(1)
+        nc.vector.reciprocal(inv_sum[:, 1:2], exp_sum[:, 1:2])
+        nc.scalar.activation(softmax_share[:], tilt[:], ACT.Copy, scale=0.5, bias=0.5)
+        nc.scalar.activation(even_share[:], tilt[:], ACT.Copy, scale=-0.5 / SLOTS, bias=0.5 / SLOTS)
+        turned_weights = [ps.tile([P, PACK, P], F32, name=f"turned_weights{b}") for b in range(HALVES)]
+        for b in range(HALVES):
+            nc.scalar.activation(
+                gain[:, b : b + 1], softmax_share[:, b : b + 1], ACT.Copy, scale=inv_sum[:, b : b + 1]
+            )
+            nc.scalar.activation(
+                weights[b][:], exps[b][:], ACT.Identity, scale=gain[:, b : b + 1], bias=even_share[:, b : b + 1]
+            )
+            for r in range(PACK):
+                nc.tensor.transpose(turned_weights[b][:, r, :], weights[b][:, r, :], identity[:])
+
+        value_grouped[0] = sb.tile([P, 2, P, 2], F32, name="value_grouped0", tag="slot_e1", align_bytes=64)
+        pick_and_turn(0, "slot_k")
+        pick_and_turn(1, "slot_m0")
+        pick_and_turn(2, "slot_r")
+
+        weight_grouped = sb.tile([P, Q, PACK], BF16, name="weight_grouped", tag="slot_v2", align_bytes=64)
+        weight_scales = sb.tile([P, Q], U8, name="weight_scales", align_bytes=64)
+        for b in range(HALVES):
+            nc.vector.tensor_tensor(
+                weight_grouped[:, b * P : (b + 1) * P, :],
+                turned_weights[b][:].rearrange("s r m -> s m r"),
+                os_cols[:].unsqueeze(1).to_broadcast([P, P, PACK]),
+                ALU.mult,
+            )
+
+        value_codes = {2: sb.tile([P, P], U32, name="value_codes2", align_bytes=64)}
+        value_scales = [sb.tile([P, n * P], U8, name=f"value_scales{j}", align_bytes=64) for j, n in enumerate((2, 1, 1))]
+
+        def quantise_values(j):
+            nc.vector.quantize_mx(
+                out=value_codes[j][:].bitcast(FP8X4),
+                scales=value_scales[j][:],
+                in_=value_grouped[j][:].rearrange("s n m u -> s (n m u)").bitcast(BF16),
+            )
+
+        def multiply(t):
+            j, n = place[t]
+            rows = slice(n * P, (n + 1) * P)
+            for b in range(HALVES):
+                cols = slice(b * P, (b + 1) * P)
+                nc.tensor.matmul_mx(
+                    out=results[b][:, t, :],
+                    lhsT=value_codes[j][:, rows].bitcast(FP8X4),
+                    lhsT_scale=value_scales[j][:, rows],
+                    rhs=weight_codes[:, cols].bitcast(FP8X4),
+                    rhs_scale=weight_scales[:, cols],
+                    start=True,
+                    stop=True,
+                )
+
+        pick_and_turn(3, "slot_w1")
+        late_codes = sb.tile([P, 2 * Q], U32, name="late_codes", tag="slot_v3", align_bytes=64)
+        weight_codes = late_codes[:, 0:Q]
+        value_codes[0] = late_codes[:, Q : 2 * Q]
+        value_codes[1] = sb.tile([P, P], U32, name="value_codes1", tag="slot_w1", align_bytes=64)
+        quantise_values(0)
+        nc.vector.quantize_mx(
+            out=weight_codes[:].bitcast(FP8X4), scales=weight_scales[:], in_=weight_grouped[:].rearrange("p q r -> p (q r)")
+        )
+        early = sb.tile([P, EARLY, Q], F32, name="early")
+        last = sb.tile([P, PACK - EARLY, Q], F32, name="last")
+        out_dealt = out_0.rearrange("(p t) q -> p t q", t=PACK)
+        multiply(0)
+        multiply(1)
+        for b in range(HALVES):
+            nc.scalar.copy(early[:, :, b * P : (b + 1) * P], results[b][:, 0:EARLY, :])
+        nc.sync.dma_start(out=out_dealt[:, 0:EARLY, :], in_=early[:])
+        quantise_values(1)
+        multiply(2)
+        quantise_values(2)
+        multiply(3)
+
+        plane_in = [sb.tile([P, P, PACK], BF16, name=f"plane_in{b}", align_bytes=64) for b in range(HALVES)]
+        plane_codes = sb.tile([P, Q], U32, name="plane_codes", align_bytes=64)
+        plane_scales = sb.tile([P, Q], U8, name="plane_scales", align_bytes=64)
+        nc.vector.tensor_copy(plane_in[0][:], results[0][:].rearrange("p t q -> p q t"))
+        nc.scalar.copy(plane_in[1][:], results[1][:].rearrange("p t q -> p q t"))
+        for b in reversed(range(HALVES)):
+            cols = slice(b * P, (b + 1) * P)
+            nc.scalar.copy(last[:, :, cols], results[b][:, EARLY:PACK, :])
+            nc.vector.quantize_mx(
+                out=plane_codes[:, cols].bitcast(FP8X4),
+                scales=plane_scales[:, cols],
+                in_=plane_in[b][:].rearrange("p q t -> p (q t)"),
+            )
+        nc.scalar.dma_start(out=out_dealt[:, EARLY:PACK, :], in_=last[:])
+        nc.sync.dma_start(out=out_1[0].rearrange("p q r -> p (q r)").bitcast(I32), in_=plane_codes[:].bitcast(I32))
+        for quad in range(4):
+            queue = nc.sync if quad % 2 == 0 else nc.scalar
+            queue.dma_start(
+                out=out_2[0, 4 * quad : 4 * quad + 4, :].bitcast(I32),
+                in_=plane_scales[32 * quad : 32 * quad + 4, :].bitcast(I32),
+            )

@@ -20,7 +20,7 @@ AX = mybir.AxisListType
 P = 128
 PACK = 4
 HALVES = Q // P
-EARLY = 2
+LAST = PACK - 1
 
 
 def tile_attend_evenbyspread_pl_kernel(tc, query, keys_words, keys_scales, th, slot_factor, vals, offs, out_0, out_1, out_2):
@@ -28,19 +28,38 @@ def tile_attend_evenbyspread_pl_kernel(tc, query, keys_words, keys_scales, th, s
     with ExitStack() as ctx:
         sb = ctx.enter_context(tc.tile_pool(name="sb", bufs=1))
         ps = ctx.enter_context(tc.psum_pool(name="ps", bufs=1))
-        ring = ctx.enter_context(tc.psum_pool(name="ring", bufs=2))
 
-        offsets = sb.tile([P, SLOTS // 16], U16, name="offsets")
-        key_scale_pool = sb.tile([P, T], U8, name="key_scale_pool", align_bytes=64)
-        key_word_pool = sb.tile([P, T], I32, name="key_word_pool", align_bytes=64)
-        query_raw = sb.tile([P, PACK, Q], F32, name="query_raw", align_bytes=64)
-        value_pools = [sb.tile([P, T], F32, name=f"value_pool{t}", tag=f"slot_v{t}", align_bytes=64) for t in range(PACK)]
-        th_cols = sb.tile([P, HALVES], F32, name="th_cols")
-        os_cols = sb.tile([P, PACK], F32, name="os_cols")
-        identity = sb.tile([P, P], F32, name="identity")
-        warm = sb.tile([P, 1], F32, name="warm")
+        def tile(shape, dtype, name, tag=None):
+            return sb.tile(shape, dtype, name=name, tag=tag or name, align_bytes=64)
+
+        def quantise(codes, scales, grouped):
+            nc.vector.quantize_mx(out=codes.bitcast(FP8X4), scales=scales, in_=grouped)
+
+        def multiply(out, lhs_codes, lhs_scales, rhs_codes, rhs_scales):
+            nc.tensor.matmul_mx(
+                out=out,
+                lhsT=lhs_codes.bitcast(FP8X4),
+                lhsT_scale=lhs_scales,
+                rhs=rhs_codes.bitcast(FP8X4),
+                rhs_scale=rhs_scales,
+                start=True,
+                stop=True,
+            )
+
+        halves = [slice(b * P, (b + 1) * P) for b in range(HALVES)]
+
+        offsets = tile([P, SLOTS // 16], U16, "offsets")
+        key_scale_pool = tile([P, T], U8, "key_scale_pool")
+        key_word_pool = tile([P, T], I32, "key_word_pool")
+        query_raw = tile([P, PACK, Q], F32, "query_raw")
+        value_pools = [tile([P, T], F32, f"value_pool{t}") for t in range(PACK)]
+        th_rows = tile([P, P], F32, "th_rows")
+        factor_cols = tile([P, PACK], F32, "factor_cols")
+        identity = tile([P, P], F32, "identity")
+        warm = tile([P, 1], F32, "warm")
 
         vals_dealt = vals.rearrange("(p t) c -> p t c", t=PACK)
+        nc.vector.memset(th_rows[:].bitcast(I32), 0)
         nc.vector.memset(key_scale_pool[:].bitcast(I32), 0)
         make_identity(nc, identity[:])
         nc.sync.dma_start(out=query_raw[:], in_=query.rearrange("(p j) q -> p j q", j=PACK))
@@ -51,68 +70,55 @@ def tile_attend_evenbyspread_pl_kernel(tc, query, keys_words, keys_scales, th, s
                 in_=keys_scales[0, 4 * quad : 4 * quad + 4, :].bitcast(I32),
             )
         nc.sync.dma_start(out=key_word_pool[:], in_=keys_words[0].rearrange("p t r -> p (t r)").bitcast(I32))
+        nc.sync.dma_start(out=th_rows[0:HALVES, :], in_=th.rearrange("(b p) o -> b (p o)", p=P))
         nc.sync.dma_start(out=value_pools[0][:], in_=vals_dealt[:, 0, :])
-        with nc.allow_non_contiguous_dma(reason="one threshold a partition"):
-            nc.sync.dma_start(out=th_cols[:], in_=th.rearrange("(b p) o -> p (b o)", p=P))
-        nc.sync.dma_start(out=value_pools[1][:], in_=vals_dealt[:, 1, :])
-        nc.sync.dma_start(out=os_cols[:], in_=slot_factor.rearrange("o (s r) -> s (o r)", r=PACK))
-        for t in range(2, PACK):
+        nc.sync.dma_start(out=factor_cols[:], in_=slot_factor.rearrange("o (s r) -> s (o r)", r=PACK))
+        for t in range(1, PACK):
             nc.sync.dma_start(out=value_pools[t][:], in_=vals_dealt[:, t, :])
         nc.scalar.activation(warm[:], identity[:, 0:1], ACT.Exp)
 
-        key_scales = sb.tile([P, SLOTS], U8, name="key_scales", align_bytes=64)
-        key_words = sb.tile([P, SLOTS], U32, name="key_words", tag="slot_k", align_bytes=64)
+        key_scales = tile([P, SLOTS], U8, "key_scales")
+        key_words = tile([P, SLOTS], U32, "key_words")
         nc.vector.tensor_copy(key_scales[:], key_scale_pool[:].indirect(offsets[:]))
 
-        query_grouped = sb.tile([P, Q, PACK], BF16, name="query_grouped", align_bytes=64)
-        query_codes = sb.tile([P, Q], U32, name="query_codes", align_bytes=64)
-        query_scales = sb.tile([P, Q], U8, name="query_scales", align_bytes=64)
+        query_grouped = tile([P, Q, PACK], BF16, "query_grouped")
+        query_codes = tile([P, Q], U32, "query_codes")
+        query_scales = tile([P, Q], U8, "query_scales")
         nc.scalar.copy(query_grouped[:], query_raw[:].rearrange("p j q -> p q j"))
-        nc.vector.quantize_mx(
-            out=query_codes[:].bitcast(FP8X4), scales=query_scales[:], in_=query_grouped[:].rearrange("p q j -> p (q j)")
-        )
+        quantise(query_codes[:], query_scales[:], query_grouped[:].rearrange("p q j -> p (q j)"))
+
+        th_bias = tile([P, HALVES], F32, "th_bias")
+        turned_th = ps.tile([P, PACK, P], F32, name="turned_th", tag="results0")
+        nc.tensor.transpose(turned_th[:, 0, :], th_rows[:], identity[:])
+        nc.scalar.activation(th_bias[:], turned_th[:, 0, 0:HALVES], ACT.Copy, scale=-2.0)
+
         scores = [ps.tile([P, SLOTS], F32, name=f"scores{b}") for b in range(HALVES)]
         run = SLOTS // 2
         for h in range(2):
             slots = slice(h * run, (h + 1) * run)
-            nc.vector.tensor_copy(
-                key_words[:, slots], key_word_pool[:].bitcast(U32).indirect(offsets[:, h * run // 16 : (h + 1) * run // 16])
-            )
+            listed = offsets[:, h * run // 16 : (h + 1) * run // 16]
+            nc.vector.tensor_copy(key_words[:, slots], key_word_pool[:].bitcast(U32).indirect(listed))
             for b in range(HALVES):
-                cols = slice(b * P, (b + 1) * P)
-                nc.tensor.matmul_mx(
-                    out=scores[b][:, slots],
-                    lhsT=query_codes[:, cols].bitcast(FP8X4),
-                    lhsT_scale=query_scales[:, cols],
-                    rhs=key_words[:, slots].bitcast(FP8X4),
-                    rhs_scale=key_scales[:, slots],
-                    start=True,
-                    stop=True,
+                multiply(
+                    scores[b][:, slots],
+                    query_codes[:, halves[b]],
+                    query_scales[:, halves[b]],
+                    key_words[:, slots],
+                    key_scales[:, slots],
                 )
 
-        results = [ps.tile([P, PACK, P], F32, name=f"results{b}") for b in range(HALVES)]
-        value_grouped = {j: sb.tile([P, 1, P, 2], F32, name=f"value_grouped{j}", align_bytes=64) for j in (1, 2)}
-        place = [(0, 0), (0, 1), (1, 0), (2, 0)]
+        neg_max = [tile([P, 1], F32, f"neg_max{b}") for b in range(HALVES)]
+        square_sum = tile([P, HALVES], F32, "square_sum")
+        exp_sum = tile([P, HALVES], F32, "exp_sum")
+        tilt = tile([P, HALVES], F32, "tilt")
+        even_share = tile([P, HALVES], F32, "even_share")
+        inv_sum = tile([P, HALVES], F32, "inv_sum")
+        gain = tile([P, HALVES], F32, "gain")
+        exps = [tile([P, PACK, P], F32, f"exps{b}") for b in range(HALVES)]
+        weights = [tile([P, PACK, P], F32, f"weights{b}") for b in range(HALVES)]
 
-        def pick_and_turn(t, tag):
-            picked = sb.tile([P, SLOTS], BF16, name=f"picked{t}", tag=tag, align_bytes=64)
-            nc.vector.tensor_copy(picked[:], value_pools[t][:].indirect(offsets[:]))
-            pairs = picked[:].bitcast(F32)
-            turned_values = ring.tile([P, 2, P], F32, name="turned_values")
-            for u in range(2):
-                nc.tensor.transpose(turned_values[:, u, :], pairs[:, u : SLOTS // 2 : 2], identity[:])
-            j, n = place[t]
-            nc.scalar.copy(value_grouped[j][:, n, :, :], turned_values[:].rearrange("s u m -> s m u"))
-
-        neg_max = [sb.tile([P, 1], F32, name=f"neg_max{b}", tag=f"slot_m{b}", align_bytes=64) for b in range(HALVES)]
-        square_sum = sb.tile([P, HALVES], F32, name="square_sum")
-        exp_sum = sb.tile([P, HALVES], F32, name="exp_sum")
-        tilt = sb.tile([P, HALVES], F32, name="tilt")
-        softmax_share = sb.tile([P, HALVES], F32, name="softmax_share")
-        even_share = sb.tile([P, HALVES], F32, name="even_share")
-        gain = sb.tile([P, HALVES], F32, name="gain")
-        exps = [sb.tile([P, PACK, P], F32, name=f"exps{b}", tag=f"slot_e{b}", align_bytes=64) for b in range(HALVES)]
-        weights = [sb.tile([P, PACK, P], F32, name=f"weights{b}", tag=f"slot_w{b}", align_bytes=64) for b in range(HALVES)]
+        def row_max(b):
+            nc.vector.tensor_reduce(neg_max[b][:], scores[b][:], AX.X, ALU.max, negate=True)
 
         def square(b):
             nc.scalar.activation(
@@ -121,9 +127,6 @@ def tile_attend_evenbyspread_pl_kernel(tc, query, keys_words, keys_scales, th, s
                 ACT.Square,
                 scale=1.0 / 16.0,
                 accum_out=square_sum[:, b : b + 1],
-            )
-            nc.scalar.activation(
-                tilt[:, b : b + 1], th_cols[:, b : b + 1], ACT.Tanh, scale=-2.0, bias=square_sum[:, b : b + 1]
             )
 
         def exponent(b):
@@ -134,105 +137,141 @@ def tile_attend_evenbyspread_pl_kernel(tc, query, keys_words, keys_scales, th, s
                 bias=neg_max[b][:],
                 accum_out=exp_sum[:, b : b + 1],
             )
+            nc.vector.reciprocal(inv_sum[:, b : b + 1], exp_sum[:, b : b + 1])
 
-        inv_sum = sb.tile([P, HALVES], F32, name="inv_sum", tag="slot_r", align_bytes=64)
-        nc.vector.tensor_reduce(neg_max[0][:], scores[0][:], AX.X, ALU.max, negate=True)
-        square(1)
-        nc.vector.tensor_reduce(neg_max[1][:], scores[1][:], AX.X, ALU.max, negate=True)
-        exponent(0)
-        nc.vector.reciprocal(inv_sum[:, 0:1], exp_sum[:, 0:1])
-        square(0)
-        exponent(1)
-        nc.vector.reciprocal(inv_sum[:, 1:2], exp_sum[:, 1:2])
-        nc.scalar.activation(softmax_share[:], tilt[:], ACT.Copy, scale=0.5, bias=0.5)
-        nc.scalar.activation(even_share[:], tilt[:], ACT.Copy, scale=-0.5 / SLOTS, bias=0.5 / SLOTS)
         turned_weights = [ps.tile([P, PACK, P], F32, name=f"turned_weights{b}") for b in range(HALVES)]
-        for b in range(HALVES):
+
+        def tilt_of(b):
+            nc.scalar.activation(tilt[:, b : b + 1], square_sum[:, b : b + 1], ACT.Tanh, bias=th_bias[:, b : b + 1])
+
+        def even_of(b):
             nc.scalar.activation(
-                gain[:, b : b + 1], softmax_share[:, b : b + 1], ACT.Copy, scale=inv_sum[:, b : b + 1]
+                even_share[:, b : b + 1], tilt[:, b : b + 1], ACT.Copy, scale=-1.0 / SLOTS, bias=1.0 / SLOTS
             )
+
+        def gain_of(b):
+            column = slice(b, b + 1)
             nc.scalar.activation(
-                weights[b][:], exps[b][:], ACT.Identity, scale=gain[:, b : b + 1], bias=even_share[:, b : b + 1]
+                gain[:, column], tilt[:, column], ACT.Identity, scale=inv_sum[:, column], bias=inv_sum[:, column]
+            )
+
+        def weigh(b):
+            column = slice(b, b + 1)
+            nc.scalar.activation(
+                weights[b][:], exps[b][:], ACT.Identity, scale=gain[:, column], bias=even_share[:, column]
             )
             for r in range(PACK):
                 nc.tensor.transpose(turned_weights[b][:, r, :], weights[b][:, r, :], identity[:])
 
-        value_grouped[0] = sb.tile([P, 2, P, 2], F32, name="value_grouped0", tag="slot_e1", align_bytes=64)
-        pick_and_turn(0, "slot_k")
-        pick_and_turn(1, "slot_m0")
-        pick_and_turn(2, "slot_r")
+        square(0)
+        row_max(1)
+        row_max(0)
+        exponent(1)
+        tilt_of(0)
+        exponent(0)
+        even_of(0)
+        square(1)
+        gain_of(0)
+        tilt_of(1)
+        weigh(0)
+        even_of(1)
+        gain_of(1)
+        weigh(1)
 
-        weight_grouped = sb.tile([P, Q, PACK], BF16, name="weight_grouped", tag="slot_v2", align_bytes=64)
-        weight_scales = sb.tile([P, Q], U8, name="weight_scales", align_bytes=64)
+        picked = {}
+
+        def pick(t, tag):
+            picked[t] = tile([P, SLOTS], BF16, f"picked{t}", tag)
+            nc.vector.tensor_copy(picked[t][:], value_pools[t][:].indirect(offsets[:]))
+
+        def turn(t, grouped, bank):
+            pairs = picked[t][:].bitcast(F32)
+            turned_values = ps.tile([P, 2, P], F32, name=f"turned_values{t}", tag=bank)
+            for u in range(2):
+                nc.tensor.transpose(turned_values[:, u, :], pairs[:, u : SLOTS // 2 : 2], identity[:])
+            nc.scalar.copy(grouped, turned_values[:].rearrange("s u m -> s m u"))
+
+        def as_bf16(grouped):
+            return grouped[:].rearrange("s m u -> s (m u)").bitcast(BF16)
+
+        weight_scales = tile([P, Q], U8, "weight_scales")
+
+        first_grouped = tile([P, 2 * P, 2], F32, "first_grouped", "exps1")
+        third_grouped = tile([P, P, 2], F32, "third_grouped")
+        last_grouped = tile([P, P, 2], F32, "last_grouped")
+        pick(0, "key_words")
+        turn(0, first_grouped[:, 0:P, :], "turned_values0")
+        pick(1, "neg_max0")
+        turn(1, first_grouped[:, P : 2 * P, :], "turned_values1")
+        pick(2, "exp_sum")
+
+        weight_grouped = tile([P, Q, PACK], BF16, "weight_grouped", "value_pool2")
         for b in range(HALVES):
-            nc.vector.tensor_tensor(
-                weight_grouped[:, b * P : (b + 1) * P, :],
+            nc.vector.scalar_tensor_tensor(
+                weight_grouped[:, halves[b], :],
                 turned_weights[b][:].rearrange("s r m -> s m r"),
-                os_cols[:].unsqueeze(1).to_broadcast([P, P, PACK]),
+                0.5,
+                factor_cols[:].unsqueeze(1).to_broadcast([P, P, PACK]),
+                ALU.mult,
                 ALU.mult,
             )
+        turn(2, third_grouped[:], "turned_weights0")
+        pick(LAST, "weights1")
+        turn(LAST, last_grouped[:], "turned_values0")
 
-        value_codes = {2: sb.tile([P, P], U32, name="value_codes2", align_bytes=64)}
-        value_scales = [sb.tile([P, n * P], U8, name=f"value_scales{j}", align_bytes=64) for j, n in enumerate((2, 1, 1))]
-
-        def quantise_values(j):
-            nc.vector.quantize_mx(
-                out=value_codes[j][:].bitcast(FP8X4),
-                scales=value_scales[j][:],
-                in_=value_grouped[j][:].rearrange("s n m u -> s (n m u)").bitcast(BF16),
-            )
-
-        def multiply(t):
-            j, n = place[t]
-            rows = slice(n * P, (n + 1) * P)
-            for b in range(HALVES):
-                cols = slice(b * P, (b + 1) * P)
-                nc.tensor.matmul_mx(
-                    out=results[b][:, t, :],
-                    lhsT=value_codes[j][:, rows].bitcast(FP8X4),
-                    lhsT_scale=value_scales[j][:, rows],
-                    rhs=weight_codes[:, cols].bitcast(FP8X4),
-                    rhs_scale=weight_scales[:, cols],
-                    start=True,
-                    stop=True,
-                )
-
-        pick_and_turn(3, "slot_w1")
-        late_codes = sb.tile([P, 2 * Q], U32, name="late_codes", tag="slot_v3", align_bytes=64)
+        late_codes = tile([P, 2 * Q], U32, "late_codes", "value_pool3")
         weight_codes = late_codes[:, 0:Q]
-        value_codes[0] = late_codes[:, Q : 2 * Q]
-        value_codes[1] = sb.tile([P, P], U32, name="value_codes1", tag="slot_w1", align_bytes=64)
-        quantise_values(0)
-        nc.vector.quantize_mx(
-            out=weight_codes[:].bitcast(FP8X4), scales=weight_scales[:], in_=weight_grouped[:].rearrange("p q r -> p (q r)")
-        )
-        early = sb.tile([P, EARLY, Q], F32, name="early")
-        last = sb.tile([P, PACK - EARLY, Q], F32, name="last")
-        out_dealt = out_0.rearrange("(p t) q -> p t q", t=PACK)
-        multiply(0)
-        multiply(1)
-        for b in range(HALVES):
-            nc.scalar.copy(early[:, :, b * P : (b + 1) * P], results[b][:, 0:EARLY, :])
-        nc.sync.dma_start(out=out_dealt[:, 0:EARLY, :], in_=early[:])
-        quantise_values(1)
-        multiply(2)
-        quantise_values(2)
-        multiply(3)
+        first_codes = late_codes[:, Q : 2 * Q]
+        first_scales = tile([P, 2 * P], U8, "first_scales")
+        quantise(weight_codes, weight_scales[:], weight_grouped[:].rearrange("p q r -> p (q r)"))
+        quantise(first_codes, first_scales[:], as_bf16(first_grouped))
+        third_codes = tile([P, P], U32, "third_codes", "weights1")
+        third_scales = tile([P, P], U8, "third_scales")
+        quantise(third_codes[:], third_scales[:], as_bf16(third_grouped))
+        last_codes = tile([P, P], U32, "last_codes")
+        last_scales = tile([P, P], U8, "last_scales")
+        quantise(last_codes[:], last_scales[:], as_bf16(last_grouped))
+        value_operands = [
+            (first_codes[:, 0:P], first_scales[:, 0:P]),
+            (first_codes[:, P : 2 * P], first_scales[:, P : 2 * P]),
+            (third_codes[:], third_scales[:]),
+            (last_codes[:], last_scales[:]),
+        ]
 
-        plane_in = [sb.tile([P, P, PACK], BF16, name=f"plane_in{b}", align_bytes=64) for b in range(HALVES)]
-        plane_codes = sb.tile([P, Q], U32, name="plane_codes", align_bytes=64)
-        plane_scales = sb.tile([P, Q], U8, name="plane_scales", align_bytes=64)
-        nc.vector.tensor_copy(plane_in[0][:], results[0][:].rearrange("p t q -> p q t"))
-        nc.scalar.copy(plane_in[1][:], results[1][:].rearrange("p t q -> p q t"))
+        out_dealt = out_0.rearrange("(p t) q -> p t q", t=PACK)
+        plane_in = [tile([P, P, PACK], BF16, f"plane_in{b}") for b in range(HALVES)]
+        plane_codes = tile([P, Q], U32, "plane_codes")
+        plane_scales = tile([P, Q], U8, "plane_scales")
+        results, staged = {}, {}
+        for pair, bank in enumerate(("results", "scores")):
+            staged[pair] = tile([P, 2, Q], F32, f"staged{pair}")
+            for b in range(HALVES):
+                results[pair, b] = ps.tile([P, 2, P], F32, name=f"results{pair}_{b}", tag=f"{bank}{b}")
+            for u in range(2):
+                codes, scales = value_operands[2 * pair + u]
+                for b in range(HALVES):
+                    multiply(
+                        results[pair, b][:, u, :], codes, scales, weight_codes[:, halves[b]], weight_scales[:, halves[b]]
+                    )
+
+        def round_pair(copy, pair, b):
+            copy(plane_in[b][:, :, 2 * pair : 2 * pair + 2], results[pair, b][:].rearrange("p u q -> p q u"))
+
+        def stage_pair(copy, pair, b):
+            copy(staged[pair][:, :, halves[b]], results[pair, b][:])
+
+        round_pair(nc.vector.tensor_copy, 0, 0)
+        stage_pair(nc.scalar.copy, 0, 1)
+        round_pair(nc.scalar.copy, 0, 1)
+        stage_pair(nc.vector.tensor_copy, 0, 0)
+        nc.sync.dma_start(out=out_dealt[:, 0:2, :], in_=staged[0][:])
+        round_pair(nc.vector.tensor_copy, 1, 0)
+        round_pair(nc.scalar.copy, 1, 1)
         for b in reversed(range(HALVES)):
-            cols = slice(b * P, (b + 1) * P)
-            nc.scalar.copy(last[:, :, cols], results[b][:, EARLY:PACK, :])
-            nc.vector.quantize_mx(
-                out=plane_codes[:, cols].bitcast(FP8X4),
-                scales=plane_scales[:, cols],
-                in_=plane_in[b][:].rearrange("p q t -> p (q t)"),
-            )
-        nc.scalar.dma_start(out=out_dealt[:, EARLY:PACK, :], in_=last[:])
+            stage_pair(nc.scalar.copy, 1, b)
+        for b in range(HALVES):
+            quantise(plane_codes[:, halves[b]], plane_scales[:, halves[b]], plane_in[b][:].rearrange("p q t -> p (q t)"))
+        nc.scalar.dma_start(out=out_dealt[:, 2:PACK, :], in_=staged[1][:])
         nc.sync.dma_start(out=out_1[0].rearrange("p q r -> p (q r)").bitcast(I32), in_=plane_codes[:].bitcast(I32))
         for quad in range(4):
             queue = nc.sync if quad % 2 == 0 else nc.scalar

from contextlib import ExitStack

import concourse.mybir as mybir
from concourse.masks import make_identity

D, E, T, SLOTS, Q = 512, 512, 2048, 512, 256
FLOPS = 2 * D * Q * SLOTS + 2 * SLOTS * E * Q

F32 = mybir.dt.float32
BF16 = mybir.dt.bfloat16
I32 = mybir.dt.int32
U32 = mybir.dt.uint32
U16 = mybir.dt.uint16
U8 = mybir.dt.uint8
FP8X4 = mybir.dt.float8_e4m3fn_x4
ACT = mybir.ActivationFunctionType
ALU = mybir.AluOpType
AX = mybir.AxisListType

P = 128
PACK = 4
HALVES = Q // P
LAST = PACK - 1


def tile_attend_evenbyspread_pl_kernel(tc, query, keys_words, keys_scales, th, slot_factor, vals, offs, out_0, out_1, out_2):
    nc = tc.nc
    with ExitStack() as ctx:
        sb = ctx.enter_context(tc.tile_pool(name="sb", bufs=1))
        ps = ctx.enter_context(tc.psum_pool(name="ps", bufs=1))

        def tile(shape, dtype, name, tag=None):
            return sb.tile(shape, dtype, name=name, tag=tag or name, align_bytes=64)

        def quantise(codes, scales, grouped):
            nc.vector.quantize_mx(out=codes.bitcast(FP8X4), scales=scales, in_=grouped)

        def multiply(out, lhs_codes, lhs_scales, rhs_codes, rhs_scales):
            nc.tensor.matmul_mx(
                out=out,
                lhsT=lhs_codes.bitcast(FP8X4),
                lhsT_scale=lhs_scales,
                rhs=rhs_codes.bitcast(FP8X4),
                rhs_scale=rhs_scales,
                start=True,
                stop=True,
            )

        halves = [slice(b * P, (b + 1) * P) for b in range(HALVES)]

        offsets = tile([P, SLOTS // 16], U16, "offsets")
        key_scale_pool = tile([P, T], U8, "key_scale_pool")
        key_word_pool = tile([P, T], I32, "key_word_pool")
        query_raw = tile([P, PACK, Q], F32, "query_raw")
        value_pools = [tile([P, T], F32, f"value_pool{t}") for t in range(PACK)]
        th_rows = tile([P, P], F32, "th_rows")
        factor_cols = tile([P, PACK], F32, "factor_cols")
        identity = tile([P, P], F32, "identity")
        warm = tile([P, 1], F32, "warm")

        vals_dealt = vals.rearrange("(p t) c -> p t c", t=PACK)
        nc.vector.memset(th_rows[:].bitcast(I32), 0)
        nc.vector.memset(key_scale_pool[:].bitcast(I32), 0)
        make_identity(nc, identity[:])
        nc.sync.dma_start(out=query_raw[:], in_=query.rearrange("(p j) q -> p j q", j=PACK))
        nc.sync.dma_start(offsets[:], offs)
        for quad in range(4):
            nc.sync.dma_start(
                out=key_scale_pool[32 * quad : 32 * quad + 4, :].bitcast(I32),
                in_=keys_scales[0, 4 * quad : 4 * quad + 4, :].bitcast(I32),
            )
        nc.sync.dma_start(out=key_word_pool[:], in_=keys_words[0].rearrange("p t r -> p (t r)").bitcast(I32))
        nc.sync.dma_start(out=th_rows[0:HALVES, :], in_=th.rearrange("(b p) o -> b (p o)", p=P))
        nc.sync.dma_start(out=value_pools[0][:], in_=vals_dealt[:, 0, :])
        nc.sync.dma_start(out=factor_cols[:], in_=slot_factor.rearrange("o (s r) -> s (o r)", r=PACK))
        for t in range(1, PACK):
            nc.sync.dma_start(out=value_pools[t][:], in_=vals_dealt[:, t, :])
        nc.scalar.activation(warm[:], identity[:, 0:1], ACT.Exp)

        key_scales = tile([P, SLOTS], U8, "key_scales")
        key_words = tile([P, SLOTS], U32, "key_words")
        nc.vector.tensor_copy(key_scales[:], key_scale_pool[:].indirect(offsets[:]))

        query_grouped = tile([P, Q, PACK], BF16, "query_grouped")
        query_codes = tile([P, Q], U32, "query_codes")
        query_scales = tile([P, Q], U8, "query_scales")
        nc.scalar.copy(query_grouped[:], query_raw[:].rearrange("p j q -> p q j"))
        quantise(query_codes[:], query_scales[:], query_grouped[:].rearrange("p q j -> p (q j)"))

        th_bias = tile([P, HALVES], F32, "th_bias")
        turned_th = ps.tile([P, PACK, P], F32, name="turned_th", tag="results0")
        nc.tensor.transpose(turned_th[:, 0, :], th_rows[:], identity[:])
        nc.scalar.activation(th_bias[:], turned_th[:, 0, 0:HALVES], ACT.Copy, scale=-2.0)

        scores = [ps.tile([P, SLOTS], F32, name=f"scores{b}") for b in range(HALVES)]
        run = SLOTS // 2
        for h in range(2):
            slots = slice(h * run, (h + 1) * run)
            listed = offsets[:, h * run // 16 : (h + 1) * run // 16]
            nc.vector.tensor_copy(key_words[:, slots], key_word_pool[:].bitcast(U32).indirect(listed))
            for b in range(HALVES):
                multiply(
                    scores[b][:, slots],
                    query_codes[:, halves[b]],
                    query_scales[:, halves[b]],
                    key_words[:, slots],
                    key_scales[:, slots],
                )

        neg_max = [tile([P, 1], F32, f"neg_max{b}") for b in range(HALVES)]
        square_sum = tile([P, HALVES], F32, "square_sum")
        exp_sum = tile([P, HALVES], F32, "exp_sum")
        tilt = tile([P, HALVES], F32, "tilt")
        even_share = tile([P, HALVES], F32, "even_share")
        inv_sum = tile([P, HALVES], F32, "inv_sum")
        gain = tile([P, HALVES], F32, "gain")
        exps = [tile([P, PACK, P], F32, f"exps{b}") for b in range(HALVES)]
        weights = [tile([P, PACK, P], F32, f"weights{b}") for b in range(HALVES)]

        def row_max(b):
            nc.vector.tensor_reduce(neg_max[b][:], scores[b][:], AX.X, ALU.max, negate=True)

        def square(b):
            nc.scalar.activation(
                weights[b][:].rearrange("p r s -> p (r s)"),
                scores[b][:],
                ACT.Square,
                scale=1.0 / 16.0,
                accum_out=square_sum[:, b : b + 1],
            )

        def exponent(b):
            nc.scalar.activation(
                exps[b][:],
                scores[b][:].rearrange("p (s r) -> p r s", r=PACK),
                ACT.Exp,
                bias=neg_max[b][:],
                accum_out=exp_sum[:, b : b + 1],
            )
            nc.vector.reciprocal(inv_sum[:, b : b + 1], exp_sum[:, b : b + 1])

        turned_weights = [ps.tile([P, PACK, P], F32, name=f"turned_weights{b}") for b in range(HALVES)]

        def tilt_of(b):
            nc.scalar.activation(tilt[:, b : b + 1], square_sum[:, b : b + 1], ACT.Tanh, bias=th_bias[:, b : b + 1])

        def even_of(b):
            nc.scalar.activation(
                even_share[:, b : b + 1], tilt[:, b : b + 1], ACT.Copy, scale=-1.0 / SLOTS, bias=1.0 / SLOTS
            )

        def gain_of(b):
            column = slice(b, b + 1)
            nc.scalar.activation(
                gain[:, column], tilt[:, column], ACT.Identity, scale=inv_sum[:, column], bias=inv_sum[:, column]
            )

        def weigh(b):
            column = slice(b, b + 1)
            nc.scalar.activation(
                weights[b][:], exps[b][:], ACT.Identity, scale=gain[:, column], bias=even_share[:, column]
            )
            for r in range(PACK):
                nc.tensor.transpose(turned_weights[b][:, r, :], weights[b][:, r, :], identity[:])

        square(0)
        row_max(1)
        row_max(0)
        exponent(1)
        tilt_of(0)
        exponent(0)
        even_of(0)
        square(1)
        gain_of(0)
        tilt_of(1)
        weigh(0)
        even_of(1)
        gain_of(1)
        weigh(1)

        picked = {}

        def pick(t, tag):
            picked[t] = tile([P, SLOTS], BF16, f"picked{t}", tag)
            nc.vector.tensor_copy(picked[t][:], value_pools[t][:].indirect(offsets[:]))

        def turn(t, grouped, bank):
            pairs = picked[t][:].bitcast(F32)
            turned_values = ps.tile([P, 2, P], F32, name=f"turned_values{t}", tag=bank)
            for u in range(2):
                nc.tensor.transpose(turned_values[:, u, :], pairs[:, u : SLOTS // 2 : 2], identity[:])
            nc.scalar.copy(grouped, turned_values[:].rearrange("s u m -> s m u"))

        def as_bf16(grouped):
            return grouped[:].rearrange("s m u -> s (m u)").bitcast(BF16)

        weight_scales = tile([P, Q], U8, "weight_scales")

        first_grouped = tile([P, 2 * P, 2], F32, "first_grouped", "exps1")
        third_grouped = tile([P, P, 2], F32, "third_grouped")
        last_grouped = tile([P, P, 2], F32, "last_grouped")
        pick(0, "key_words")
        turn(0, first_grouped[:, 0:P, :], "turned_values0")
        pick(1, "neg_max0")
        turn(1, first_grouped[:, P : 2 * P, :], "turned_values1")
        pick(2, "exp_sum")

        weight_grouped = tile([P, Q, PACK], BF16, "weight_grouped", "value_pool2")
        for b in range(HALVES):
            nc.vector.scalar_tensor_tensor(
                weight_grouped[:, halves[b], :],
                turned_weights[b][:].rearrange("s r m -> s m r"),
                0.5,
                factor_cols[:].unsqueeze(1).to_broadcast([P, P, PACK]),
                ALU.mult,
                ALU.mult,
            )
        turn(2, third_grouped[:], "turned_weights0")
        pick(LAST, "weights1")
        turn(LAST, last_grouped[:], "turned_values0")

        late_codes = tile([P, 2 * Q], U32, "late_codes", "value_pool3")
        weight_codes = late_codes[:, 0:Q]
        first_codes = late_codes[:, Q : 2 * Q]
        first_scales = tile([P, 2 * P], U8, "first_scales")
        quantise(weight_codes, weight_scales[:], weight_grouped[:].rearrange("p q r -> p (q r)"))
        quantise(first_codes, first_scales[:], as_bf16(first_grouped))
        third_codes = tile([P, P], U32, "third_codes", "weights1")
        third_scales = tile([P, P], U8, "third_scales")
        quantise(third_codes[:], third_scales[:], as_bf16(third_grouped))
        last_codes = tile([P, P], U32, "last_codes")
        last_scales = tile([P, P], U8, "last_scales")
        quantise(last_codes[:], last_scales[:], as_bf16(last_grouped))
        value_operands = [
            (first_codes[:, 0:P], first_scales[:, 0:P]),
            (first_codes[:, P : 2 * P], first_scales[:, P : 2 * P]),
            (third_codes[:], third_scales[:]),
            (last_codes[:], last_scales[:]),
        ]

        out_dealt = out_0.rearrange("(p t) q -> p t q", t=PACK)
        plane_in = [tile([P, P, PACK], BF16, f"plane_in{b}") for b in range(HALVES)]
        plane_codes = tile([P, Q], U32, "plane_codes")
        plane_scales = tile([P, Q], U8, "plane_scales")
        results, staged = {}, {}
        for pair, bank in enumerate(("results", "scores")):
            staged[pair] = tile([P, 2, Q], F32, f"staged{pair}")
            for b in range(HALVES):
                results[pair, b] = ps.tile([P, 2, P], F32, name=f"results{pair}_{b}", tag=f"{bank}{b}")
            for u in range(2):
                codes, scales = value_operands[2 * pair + u]
                for b in range(HALVES):
                    multiply(
                        results[pair, b][:, u, :], codes, scales, weight_codes[:, halves[b]], weight_scales[:, halves[b]]
                    )

        def round_pair(copy, pair, b):
            copy(plane_in[b][:, :, 2 * pair : 2 * pair + 2], results[pair, b][:].rearrange("p u q -> p q u"))

        def stage_pair(copy, pair, b):
            copy(staged[pair][:, :, halves[b]], results[pair, b][:])

        round_pair(nc.vector.tensor_copy, 0, 0)
        stage_pair(nc.scalar.copy, 0, 1)
        round_pair(nc.scalar.copy, 0, 1)
        stage_pair(nc.vector.tensor_copy, 0, 0)
        nc.sync.dma_start(out=out_dealt[:, 0:2, :], in_=staged[0][:])
        round_pair(nc.vector.tensor_copy, 1, 0)
        round_pair(nc.scalar.copy, 1, 1)
        for b in reversed(range(HALVES)):
            stage_pair(nc.scalar.copy, 1, b)
        for b in range(HALVES):
            quantise(plane_codes[:, halves[b]], plane_scales[:, halves[b]], plane_in[b][:].rearrange("p q t -> p (q t)"))
        nc.scalar.dma_start(out=out_dealt[:, 2:PACK, :], in_=staged[1][:])
        nc.sync.dma_start(out=out_1[0].rearrange("p q r -> p (q r)").bitcast(I32), in_=plane_codes[:].bitcast(I32))
        for quad in range(4):
            queue = nc.sync if quad % 2 == 0 else nc.scalar
            queue.dma_start(
                out=out_2[0, 4 * quad : 4 * quad + 4, :].bitcast(I32),
                in_=plane_scales[32 * quad : 32 * quad + 4, :].bitcast(I32),
            )
